import numpy as np
import ml_dtypes


def mxq(x, axis, fmt="e4m3"):
    dtype, down = {"e4m3": (ml_dtypes.float8_e4m3fn, 7), "e5m2": (ml_dtypes.float8_e5m2, 14)}[fmt]
    v = np.moveaxis(np.asarray(x, np.float32).astype(ml_dtypes.bfloat16).astype(np.float64), axis, -1)
    blocks = v.reshape(v.shape[:-1] + (-1, 32))
    amax = np.abs(blocks).max(-1, keepdims=True)
    byte = np.maximum(np.where(amax > 0, np.frexp(amax)[1] - 1 + 127, 0) - down, 1)
    scale = np.exp2(byte - 127.0)
    codes = (blocks / scale).astype(np.float32).astype(dtype).astype(np.float64)
    return np.moveaxis((codes * scale).reshape(v.shape), -1, axis)


WIDE = False


def mx_kscale(k):
    if not WIDE:
        return np.ones(k)
    levels = np.array([30, -30])
    if k % 512:
        return np.exp2(np.random.permutation(np.resize(levels, k // 32))).repeat(32)
    a = np.empty((k // 512, 16))
    for p in range(k // 512):
        a[p, :8] = np.random.permutation(np.resize(levels, 8))
        for g in range(8):
            far = levels[np.abs(levels - a[p, g]) >= 10]
            a[p, g + 8] = far[np.random.randint(len(far))]
    return np.exp2(a.ravel()).repeat(32)


def f64(x):
    return np.asarray(x).astype(np.float64)


def striped(idx):
    return np.tile(np.asarray(idx).reshape(-1, 16).T, (8, 1)).astype(np.uint16)


def unstriped(offs):
    return offs[:16].T.reshape(-1).astype(np.int64)


E2M1 = np.array([0.0, 0.5, 1.0, 1.5, 2.0, 3.0, 4.0, 6.0, -0.0, -0.5, -1.0, -1.5, -2.0, -3.0, -4.0, -6.0])


def pack_weight(w, fmt):
    k, n = w.shape
    w = f64(np.asarray(w, np.float32).astype(ml_dtypes.bfloat16)).reshape(k // 32, 32, n)
    amax = np.abs(w).max(1)
    if fmt in ("e4m3", "e5m2"):
        byte = np.frexp(amax)[1] - 1 + 127 - (7 if fmt == "e4m3" else 14)
    else:
        mant, ex = np.frexp(amax / 6.0)
        byte = np.where(mant > 0.5, ex, ex - 1) + 127
    byte = np.clip(np.where(amax > 0, byte, 1), 1, 254)
    scaled = (w * np.exp2(127.0 - byte)[:, None, :]).reshape(k, n).astype(np.float32)
    by_word = np.ascontiguousarray(scaled.reshape(k // 512, 128, 4, n).transpose(0, 1, 3, 2))
    if fmt in ("e4m3", "e5m2"):
        words = by_word.astype(ml_dtypes.float8_e4m3fn if fmt == "e4m3" else ml_dtypes.float8_e5m2).view(np.uint8)
    else:
        c = by_word.astype(ml_dtypes.float4_e2m1fn).view(np.uint8) & 0xF
        words = (c[..., 0::2] | (c[..., 1::2] << 4)).reshape(k // 512, 128, 2 * n)
    return np.ascontiguousarray(words), np.ascontiguousarray(byte.astype(np.uint8).reshape(k // 512, 16, n))


def unpack_weight(words, scales, fmt):
    g, _, n = scales.shape
    words = np.ascontiguousarray(words).reshape(g, 128, n, -1)
    if fmt in ("e4m3", "e5m2"):
        vals = words.view(ml_dtypes.float8_e4m3fn if fmt == "e4m3" else ml_dtypes.float8_e5m2).astype(np.float64)
    else:
        nib = np.empty((g, 128, n, 4), np.uint8)
        nib[..., 0::2] = words & 0xF
        nib[..., 1::2] = words >> 4
        vals = E2M1[nib]
    vals = vals * np.repeat(np.exp2(scales.astype(np.float64) - 127.0), 8, axis=1)[..., None]
    return vals.transpose(0, 1, 3, 2).reshape(g * 512, n)


def bf(x):
    return np.asarray(x, np.float32).astype(ml_dtypes.bfloat16)


def planes(Y):
    r, m = Y.shape
    b = f64(bf(Y)).reshape(r // 32, 32, m)
    amax = np.abs(b).max(1)
    byte = np.clip(np.where(amax > 0, np.frexp(amax)[1] - 1 + 127 - 7, 1), 1, 254)
    codes = (b * np.exp2(127.0 - byte)[:, None, :]).reshape(r, m).astype(np.float32).astype(ml_dtypes.float8_e4m3fn).view(np.uint8)
    words = codes.reshape(r // 512, 128, 4, m).transpose(0, 1, 3, 2)
    return np.ascontiguousarray(words), np.ascontiguousarray(byte.astype(np.uint8).reshape(r // 512, 16, m))


K, T, J, R, C, O, N, L = 512, 2048, 256, 512, 512, 256, 512, 512


def setup_inputs():
    n = np.random.standard_normal
    idx = np.random.permutation(T)[:J]
    idx2 = np.random.permutation(T)[:J]
    idx3 = np.random.permutation(C)[:J]
    idx4 = np.random.permutation(C)[:J]
    idx5 = np.random.permutation(C)[:O]
    idx6 = np.random.permutation(C)[:O]
    fk = mx_kscale(K)
    fr = mx_kscale(R)
    fl = mx_kscale(L)
    xtp = pack_weight(n((K, T)) / fk[:, None], "e4m3")
    wp = pack_weight(n((K, R)) * 1 / np.sqrt(K) * fk[:, None] * fr, "e2m1")
    w2p = pack_weight(n((K, R)) * 1 / np.sqrt(K) * fk[:, None] * fr, "e5m2")
    wbp = pack_weight(n((R, N)) * 1 / np.sqrt(R) / fr[:, None], "e5m2")
    sxp = pack_weight(n((L, O)) / fl[:, None], "e2m1")
    wsp = pack_weight(n((L, N)) * 1 / np.sqrt(L) * fl[:, None], "e5m2")
    return {
        "xt_words": xtp[0],
        "xt_scales": xtp[1],
        "w_words": wp[0],
        "w_scales": wp[1],
        "w2_words": w2p[0],
        "w2_scales": w2p[1],
        "wb_words": wbp[0],
        "wb_scales": wbp[1],
        "sx_words": sxp[0],
        "sx_scales": sxp[1],
        "ws_words": wsp[0],
        "ws_scales": wsp[1],
        "offs": striped(idx),
        "offs2": striped(idx2),
        "offs3": striped(idx3),
        "offs4": striped(idx4),
        "offs5": striped(idx5),
        "offs6": striped(idx6),
    }


def reference(xt_words, xt_scales, w_words, w_scales, w2_words, w2_scales, wb_words, wb_scales, sx_words, sx_scales, ws_words, ws_scales, offs, offs2, offs3, offs4, offs5, offs6):
    idx = unstriped(offs)
    idx2 = unstriped(offs2)
    idx3 = unstriped(offs3)
    idx4 = unstriped(offs4)
    idx5 = unstriped(offs5)
    idx6 = unstriped(offs6)
    xtu = unpack_weight(xt_words, xt_scales, "e4m3")
    wu = unpack_weight(w_words, w_scales, "e2m1")
    w2u = unpack_weight(w2_words, w2_scales, "e5m2")
    wbu = unpack_weight(wb_words, wb_scales, "e5m2")
    sxu = unpack_weight(sx_words, sx_scales, "e2m1")
    wsu = unpack_weight(ws_words, ws_scales, "e5m2")
    xtidxg = xtu[:, idx]
    a = wu.T @ xtidxg
    xtidx2g = xtu[:, idx2]
    b = w2u.T @ xtidx2g
    pw = np.zeros((R, C))
    pw[:, idx3] = a
    pv = np.zeros((R, C))
    pv[:, idx4] = b
    hid = np.abs(pw[:, idx5] - pv[:, idx6])
    hidq = mxq(hid, 0, "e4m3")
    y = wbu.T @ hidq + wsu.T @ sxu
    words, scales = planes(y)
    return y, words, scales

@@ -1,0 +1,229 @@
+from contextlib import ExitStack
+
+import concourse.mybir as mybir
+
+F32 = mybir.dt.float32
+BF16 = mybir.dt.bfloat16
+I32 = mybir.dt.int32
+U32 = mybir.dt.uint32
+U16 = mybir.dt.uint16
+U8 = mybir.dt.uint8
+E4M3 = mybir.dt.float8_e4m3fn_x4
+E5M2 = mybir.dt.float8_e5m2_x4
+E2M1 = mybir.dt.float4_e2m1fn_x4
+ACT = mybir.ActivationFunctionType
+ALU = mybir.AluOpType
+
+P = 128
+PACK = 4
+TOKENS, SLOTS, BOARD, READS, WIDTH = 2048, 256, 512, 256, 512
+HALF = READS // 2
+FLOPS = 536870912
+
+
+def tile_list_ahead_twoboards_skip_plain_pl_kernel(
+    tc, xt_words, xt_scales, w_words, w_scales, w2_words, w2_scales, wb_words, wb_scales,
+    sx_words, sx_scales, ws_words, ws_scales, offs, offs2, offs3, offs4, offs5, offs6,
+    out_0, out_1, out_2,
+):
+    nc = tc.nc
+    with ExitStack() as ctx:
+        sb = ctx.enter_context(tc.tile_pool(name="sb", bufs=1))
+        ps = ctx.enter_context(tc.psum_pool(name="ps", bufs=1))
+
+        def tile(name, shape, dtype):
+            return sb.tile(shape, dtype, name=name, align_bytes=64)
+
+        def load_list(name, src):
+            dst = sb.tile([P, 16], U16, name=name)
+            nc.sync.dma_start(dst[:], src)
+            return dst
+
+        def load_words(dst, src):
+            nc.sync.dma_start(dst.bitcast(I32), src.bitcast(I32))
+
+        def words8(src):
+            return src[0].rearrange("p n t -> p (n t)")
+
+        def load_plane(dst, src):
+            for r in range(4):
+                nc.sync.dma_start(dst[r:P:32, :].bitcast(I32), src[0, r:16:4, :].bitcast(I32))
+
+        def deal(copy, dst, src, run):
+            copy(
+                dst.rearrange("p t (c i) -> p c t i", i=run),
+                src.rearrange("p (c i t) -> p c t i", i=run, t=PACK),
+            )
+
+        def shared(name, shape, dtype, tag):
+            return sb.tile(shape, dtype, name=name, tag=tag, align_bytes=64)
+
+        xt_plane = tile("xt_plane", [P, TOKENS], U8)
+        w_plane = tile("w_plane", [P, WIDTH], U8)
+        w2_plane = tile("w2_plane", [P, WIDTH], U8)
+        ws_plane = tile("ws_plane", [P, WIDTH], U8)
+        wb_plane = tile("wb_plane", [P, WIDTH], U8)
+        sx_plane = tile("sx_plane", [P, READS], U8)
+        nc.gpsimd.memset(w_plane[:].bitcast(I32), 0)
+        nc.vector.memset(xt_plane[:, : TOKENS // 2].bitcast(I32), 0)
+        nc.gpsimd.memset(xt_plane[:, TOKENS // 2 :].bitcast(I32), 0)
+        for plane in (w2_plane, ws_plane, wb_plane, sx_plane):
+            nc.vector.memset(plane[:].bitcast(I32), 0)
+        pw = [tile("pw%d" % t, [P, BOARD], F32) for t in range(PACK)]
+        pv = [tile("pv%d" % t, [P, BOARD], F32) for t in range(PACK)]
+        for t in range(PACK):
+            clearer = nc.gpsimd if t == PACK - 1 else nc.vector
+            clearer.memset(pw[t][:], 0.0)
+            clearer.memset(pv[t][:], 0.0)
+
+        w_raw = tile("w_raw", [P, WIDTH], U16)
+        xt = tile("xt", [P, TOKENS], U32)
+        w2_raw = tile("w2_raw", [P, WIDTH], U32)
+        ws_raw = tile("ws_raw", [P, WIDTH], U32)
+        wb_raw = tile("wb_raw", [P, WIDTH], U32)
+        sx = tile("sx", [P, READS], U16)
+        list1 = load_list("list1", offs)
+        load_words(w_raw[:], w_words[0])
+        list3 = load_list("list3", offs3)
+        load_plane(w_plane, w_scales)
+        load_words(xt[:], words8(xt_words))
+        load_plane(xt_plane, xt_scales)
+        list2 = load_list("list2", offs2)
+        load_words(w2_raw[:], words8(w2_words))
+        load_plane(w2_plane, w2_scales)
+        list5 = load_list("list5", offs5)
+        list4 = load_list("list4", offs4)
+        list6 = load_list("list6", offs6)
+        load_words(ws_raw[:], words8(ws_words))
+        load_words(wb_raw[:], words8(wb_words))
+        load_plane(ws_plane, ws_scales)
+        load_plane(wb_plane, wb_scales)
+        load_words(sx[:], sx_words[0])
+        load_plane(sx_plane, sx_scales)
+
+        w_dealt = shared("w_dealt", [P, PACK, P], U16, "dealt_a")
+        w_plane_dealt = tile("w_plane_dealt", [P, PACK, P], U8)
+        deal(nc.scalar.copy, w_dealt[:], w_raw[:], 8)
+        deal(nc.vector.tensor_copy, w_plane_dealt[:], w_plane[:], 16)
+        x1 = tile("x1", [P, SLOTS], U32)
+        x1_plane = tile("x1_plane", [P, SLOTS], U8)
+        nc.vector.tensor_copy(x1[:], xt[:].indirect(list1[:]))
+        nc.vector.tensor_copy(x1_plane[:], xt_plane[:].indirect(list1[:]))
+        w2_dealt = shared("w2_dealt", [P, PACK, P], U32, "dealt_b")
+        deal(nc.scalar.copy, w2_dealt[:], w2_raw[:], 4)
+        x2 = tile("x2", [P, SLOTS], U32)
+        x2_plane = tile("x2_plane", [P, SLOTS], U8)
+        nc.vector.tensor_copy(x2[:], xt[:].indirect(list2[:]))
+        nc.vector.tensor_copy(x2_plane[:], xt_plane[:].indirect(list2[:]))
+        w2_plane_dealt = tile("w2_plane_dealt", [P, PACK, P], U8)
+        deal(nc.vector.tensor_copy, w2_plane_dealt[:], w2_plane[:], 16)
+
+        a = [tile("a%d" % t, [P, SLOTS], F32) for t in range(PACK)]
+        b = [shared("b%d" % t, [P, SLOTS], F32, "b%d" % t) for t in range(PACK)]
+        pw_read = [tile("pw_read%d" % t, [P, READS], F32) for t in range(PACK)]
+        diff = tile("diff", [P, PACK, READS], F32)
+
+        def scalar_copy(dst, src):
+            nc.scalar.activation(dst, src, ACT.Copy)
+
+        def product_a(t, tag):
+            acc = ps.tile([P, SLOTS], F32, name="a_ps%d" % t, tag=tag)
+            nc.tensor.matmul_mx(
+                acc[:], w_dealt[:, t, :].bitcast(E2M1), w_plane_dealt[:, t, :],
+                x1[:].bitcast(E4M3), x1_plane[:], start=True, stop=True,
+            )
+            scalar_copy(a[t][:], acc[:])
+
+        def product_b(t, copy):
+            acc = ps.tile([P, SLOTS], F32, name="b_ps%d" % t, tag="bank%d" % t)
+            nc.tensor.matmul_mx(
+                acc[:], w2_dealt[:, t, :].bitcast(E5M2), w2_plane_dealt[:, t, :],
+                x2[:].bitcast(E4M3), x2_plane[:], start=True, stop=True,
+            )
+            copy(b[t][:], acc[:])
+
+        def board_a(t):
+            scalar_copy(pw[t][:].indirect(list3[:]), a[t][:])
+            scalar_copy(pw_read[t][:], pw[t][:].indirect(list5[:]))
+
+        def board_b(t):
+            nc.vector.tensor_copy(pv[t][:].indirect(list4[:]), b[t][:])
+            if t < PACK - 1:
+                nc.vector.tensor_tensor(diff[:, t, :], pv[t][:].indirect(list6[:]), pw_read[t][:], ALU.subtract)
+
+        product_a(0, "bank_a0")
+        board_a(0)
+        product_b(0, nc.vector.tensor_copy)
+        for t in range(1, PACK):
+            product_b(t, scalar_copy)
+        for t in range(1, PACK):
+            product_a(t, "bank%d" % t)
+        board_a(1)
+        board_a(2)
+        board_a(3)
+        board_b(0)
+        board_b(1)
+        ws_dealt = shared("ws_dealt", [P, PACK, P], U32, "dealt_a")
+        wb_dealt = shared("wb_dealt", [P, PACK, P], U32, "dealt_b")
+        deal(nc.vector.tensor_copy, ws_dealt[:], ws_raw[:], 4)
+        deal(nc.vector.tensor_copy, wb_dealt[:], wb_raw[:], 4)
+        late_planes = shared("late_planes", [P, 2, PACK, P], U8, "b1")
+        ws_plane_dealt = late_planes[:, 0]
+        wb_plane_dealt = late_planes[:, 1]
+        deal(nc.vector.tensor_copy, ws_plane_dealt, ws_plane[:], 16)
+        deal(nc.vector.tensor_copy, wb_plane_dealt, wb_plane[:], 16)
+        board_b(2)
+        board_b(3)
+
+        halves = [slice(h * HALF, (h + 1) * HALF) for h in range(2)]
+        y_ps = [ps.tile([P, PACK, HALF], F32, name="y_ps%d" % h) for h in range(2)]
+        for h in range(2):
+            for t in range(PACK):
+                nc.tensor.matmul_mx(
+                    y_ps[h][:, t, :], ws_dealt[:, t, :].bitcast(E5M2), ws_plane_dealt[:, t, :],
+                    sx[:, halves[h]].bitcast(E2M1), sx_plane[:, halves[h]], start=(t == 0), stop=False,
+                )
+
+        last = PACK - 1
+        for h in range(2):
+            nc.vector.tensor_tensor(
+                diff[:, last, halves[h]], pv[last][:].indirect(list6[:, 8 * h : 8 * h + 8]),
+                pw_read[last][:, halves[h]], ALU.subtract,
+            )
+        hid = [tile("hid%d" % h, [P, HALF, PACK], BF16) for h in range(2)]
+        for h in range(2):
+            nc.scalar.activation(
+                hid[h][:].rearrange("p (c i) t -> p c t i", i=4),
+                diff[:, :, halves[h]].rearrange("p t (c i) -> p c t i", i=4),
+                ACT.Abs,
+            )
+        for h in range(2):
+            hid_codes = tile("hid_codes%d" % h, [P, HALF], U32)
+            hid_plane = tile("hid_plane%d" % h, [P, HALF], U8)
+            nc.vector.quantize_mx(
+                hid_codes[:].bitcast(E4M3), hid_plane[:], hid[h][:].rearrange("p o t -> p (o t)")
+            )
+            for t in range(PACK):
+                nc.tensor.matmul_mx(
+                    y_ps[h][:, t, :], wb_dealt[:, t, :].bitcast(E5M2), wb_plane_dealt[:, t, :],
+                    hid_codes[:].bitcast(E4M3), hid_plane[:], start=False, stop=(t == last),
+                )
+
+        y_codes = tile("y_codes", [P, READS], U32)
+        y_plane = tile("y_plane", [P, READS], U8)
+        out_rows = out_0.rearrange("(p t) o -> p t o", t=PACK)
+        out_words = out_1[0].rearrange("p o t -> p (o t)").bitcast(I32)
+        for h in range(2):
+            y_bf = tile("y_bf%d" % h, [P, HALF, PACK], BF16)
+            y = tile("y%d" % h, [P, PACK, HALF], F32)
+            scalar_copy(y[:], y_ps[h][:])
+            nc.vector.tensor_copy(
+                y_bf[:].rearrange("p (c i) t -> p c t i", i=4), y[:].rearrange("p t (c i) -> p c t i", i=4)
+            )
+            nc.vector.quantize_mx(
+                y_codes[:, halves[h]].bitcast(E4M3), y_plane[:, halves[h]], y_bf[:].rearrange("p o t -> p (o t)")
+            )
+            nc.scalar.dma_start(out_rows[:, :, halves[h]], y[:])
+            nc.sync.dma_start(out_words[:, halves[h]], y_codes[:, halves[h]].bitcast(I32))
+        for r in range(4):
+            nc.sync.dma_start(out_2[0, r:16:4, :].bitcast(I32), y_plane[r:P:32, :].bitcast(I32))

@@ -62,7 +62,7 @@ def tile_list_ahead_twoboards_skip_plain_pl_kernel(
         w_plane = tile("w_plane", [P, WIDTH], U8)
         w2_plane = tile("w2_plane", [P, WIDTH], U8)
         ws_plane = tile("ws_plane", [P, WIDTH], U8)
-        wb_plane = tile("wb_plane", [P, WIDTH], U8)
+        wb_plane = shared("wb_plane", [P, WIDTH], U8, "b02")
         sx_plane = tile("sx_plane", [P, READS], U8)
         nc.gpsimd.memset(w_plane[:].bitcast(I32), 0)
         nc.vector.memset(xt_plane[:, : TOKENS // 2].bitcast(I32), 0)
@@ -72,9 +72,9 @@ def tile_list_ahead_twoboards_skip_plain_pl_kernel(
         pw = [tile("pw%d" % t, [P, BOARD], F32) for t in range(PACK)]
         pv = [tile("pv%d" % t, [P, BOARD], F32) for t in range(PACK)]
         for t in range(PACK):
-            clearer = nc.gpsimd if t == PACK - 1 else nc.vector
-            clearer.memset(pw[t][:], 0.0)
-            clearer.memset(pv[t][:], 0.0)
+            nc.vector.memset(pw[t][:], 0.0)
+        for t in range(PACK):
+            (nc.vector if t < 2 else nc.gpsimd).memset(pv[t][:], 0.0)
 
         w_raw = tile("w_raw", [P, WIDTH], U16)
         xt = tile("xt", [P, TOKENS], U32)
@@ -90,111 +90,123 @@ def tile_list_ahead_twoboards_skip_plain_pl_kernel(
         load_plane(xt_plane, xt_scales)
         list2 = load_list("list2", offs2)
         load_words(w2_raw[:], words8(w2_words))
+        load_words(ws_raw[:], words8(ws_words))
         load_plane(w2_plane, w2_scales)
         list5 = load_list("list5", offs5)
         list4 = load_list("list4", offs4)
         list6 = load_list("list6", offs6)
-        load_words(ws_raw[:], words8(ws_words))
         load_words(wb_raw[:], words8(wb_words))
         load_plane(ws_plane, ws_scales)
         load_plane(wb_plane, wb_scales)
         load_words(sx[:], sx_words[0])
         load_plane(sx_plane, sx_scales)
 
-        w_dealt = shared("w_dealt", [P, PACK, P], U16, "dealt_a")
-        w_plane_dealt = tile("w_plane_dealt", [P, PACK, P], U8)
+        w_dealt = tile("w_dealt", [P, PACK, P], U16)
+        w2_dealt = tile("w2_dealt", [P, PACK, P], U32)
+        ws_dealt = tile("ws_dealt", [P, PACK, P], U32)
         deal(nc.scalar.copy, w_dealt[:], w_raw[:], 8)
-        deal(nc.vector.tensor_copy, w_plane_dealt[:], w_plane[:], 16)
+        deal(nc.scalar.copy, w2_dealt[:], w2_raw[:], 4)
+        deal(nc.scalar.copy, ws_dealt[:], ws_raw[:], 4)
         x1 = tile("x1", [P, SLOTS], U32)
         x1_plane = tile("x1_plane", [P, SLOTS], U8)
-        nc.vector.tensor_copy(x1[:], xt[:].indirect(list1[:]))
-        nc.vector.tensor_copy(x1_plane[:], xt_plane[:].indirect(list1[:]))
-        w2_dealt = shared("w2_dealt", [P, PACK, P], U32, "dealt_b")
-        deal(nc.scalar.copy, w2_dealt[:], w2_raw[:], 4)
         x2 = tile("x2", [P, SLOTS], U32)
         x2_plane = tile("x2_plane", [P, SLOTS], U8)
-        nc.vector.tensor_copy(x2[:], xt[:].indirect(list2[:]))
+        w_plane_dealt = tile("w_plane_dealt", [P, PACK, P], U8)
+        deal(nc.vector.tensor_copy, w_plane_dealt[:], w_plane[:], 16)
+        nc.vector.tensor_copy(x1_plane[:], xt_plane[:].indirect(list1[:]))
+        nc.vector.tensor_copy(x1[:], xt[:].indirect(list1[:]))
         nc.vector.tensor_copy(x2_plane[:], xt_plane[:].indirect(list2[:]))
-        w2_plane_dealt = tile("w2_plane_dealt", [P, PACK, P], U8)
-        deal(nc.vector.tensor_copy, w2_plane_dealt[:], w2_plane[:], 16)
-
-        a = [tile("a%d" % t, [P, SLOTS], F32) for t in range(PACK)]
-        b = [shared("b%d" % t, [P, SLOTS], F32, "b%d" % t) for t in range(PACK)]
-        pw_read = [tile("pw_read%d" % t, [P, READS], F32) for t in range(PACK)]
-        diff = tile("diff", [P, PACK, READS], F32)
+        nc.vector.tensor_copy(x2[:], xt[:].indirect(list2[:]))
 
         def scalar_copy(dst, src):
             nc.scalar.activation(dst, src, ACT.Copy)
 
-        def product_a(t, tag):
-            acc = ps.tile([P, SLOTS], F32, name="a_ps%d" % t, tag=tag)
+        def product_a(acc, t):
             nc.tensor.matmul_mx(
-                acc[:], w_dealt[:, t, :].bitcast(E2M1), w_plane_dealt[:, t, :],
+                acc, w_dealt[:, t, :].bitcast(E2M1), w_plane_dealt[:, t, :],
                 x1[:].bitcast(E4M3), x1_plane[:], start=True, stop=True,
             )
-            scalar_copy(a[t][:], acc[:])
 
-        def product_b(t, copy):
-            acc = ps.tile([P, SLOTS], F32, name="b_ps%d" % t, tag="bank%d" % t)
+        def product_b(acc, t):
             nc.tensor.matmul_mx(
-                acc[:], w2_dealt[:, t, :].bitcast(E5M2), w2_plane_dealt[:, t, :],
+                acc, w2_dealt[:, t, :].bitcast(E5M2), w2_plane_dealt[:, t, :],
                 x2[:].bitcast(E4M3), x2_plane[:], start=True, stop=True,
             )
-            copy(b[t][:], acc[:])
 
-        def board_a(t):
-            scalar_copy(pw[t][:].indirect(list3[:]), a[t][:])
-            scalar_copy(pw_read[t][:], pw[t][:].indirect(list5[:]))
-
-        def board_b(t):
-            nc.vector.tensor_copy(pv[t][:].indirect(list4[:]), b[t][:])
-            if t < PACK - 1:
-                nc.vector.tensor_tensor(diff[:, t, :], pv[t][:].indirect(list6[:]), pw_read[t][:], ALU.subtract)
-
-        product_a(0, "bank_a0")
-        board_a(0)
-        product_b(0, nc.vector.tensor_copy)
-        for t in range(1, PACK):
-            product_b(t, scalar_copy)
-        for t in range(1, PACK):
-            product_a(t, "bank%d" % t)
-        board_a(1)
-        board_a(2)
-        board_a(3)
-        board_b(0)
-        board_b(1)
-        ws_dealt = shared("ws_dealt", [P, PACK, P], U32, "dealt_a")
-        wb_dealt = shared("wb_dealt", [P, PACK, P], U32, "dealt_b")
-        deal(nc.vector.tensor_copy, ws_dealt[:], ws_raw[:], 4)
-        deal(nc.vector.tensor_copy, wb_dealt[:], wb_raw[:], 4)
-        late_planes = shared("late_planes", [P, 2, PACK, P], U8, "b1")
-        ws_plane_dealt = late_planes[:, 0]
-        wb_plane_dealt = late_planes[:, 1]
-        deal(nc.vector.tensor_copy, ws_plane_dealt, ws_plane[:], 16)
-        deal(nc.vector.tensor_copy, wb_plane_dealt, wb_plane[:], 16)
-        board_b(2)
-        board_b(3)
-
+        a0_ps = ps.tile([P, SLOTS], F32, name="a0_ps", tag="first")
+        a1_ps = ps.tile([P, SLOTS], F32, name="a1_ps")
+        a23_ps = ps.tile([P, 2, SLOTS], F32, name="a23_ps")
+        b02_ps = ps.tile([P, 2, SLOTS], F32, name="b02_ps")
+        b13_ps = ps.tile([P, 2, SLOTS], F32, name="b13_ps")
+        a0 = tile("a0", [P, SLOTS], F32)
+        a1 = shared("a1", [P, SLOTS], F32, "a1")
+        a23 = tile("a23", [P, 2, SLOTS], F32)
+        b13 = tile("b13", [P, 2, SLOTS], F32)
+        read = [tile("read%d" % t, [P, READS], F32) for t in range(PACK)]
         halves = [slice(h * HALF, (h + 1) * HALF) for h in range(2)]
-        y_ps = [ps.tile([P, PACK, HALF], F32, name="y_ps%d" % h) for h in range(2)]
+
+        product_a(a0_ps[:], 0)
+        product_a(a1_ps[:], 1)
+        product_a(a23_ps[:, 0, :], 2)
+        product_a(a23_ps[:, 1, :], 3)
+        scalar_copy(a0[:], a0_ps[:])
+        scalar_copy(pw[0][:].indirect(list3[:]), a0[:])
+        nc.vector.tensor_copy(a1[:], a1_ps[:])
+        nc.vector.tensor_copy(pw[1][:].indirect(list3[:]), a1[:])
+        w2_plane_dealt = shared("w2_plane_dealt", [P, PACK, P], U8, "a1")
+        deal(nc.vector.tensor_copy, w2_plane_dealt[:], w2_plane[:], 16)
+        scalar_copy(a23[:], a23_ps[:])
+        scalar_copy(pw[2][:].indirect(list3[:]), a23[:, 0, :])
+        nc.vector.tensor_copy(pw[3][:].indirect(list3[:]), a23[:, 1, :])
+
+        product_b(b02_ps[:, 0, :], 0)
+        product_b(b02_ps[:, 1, :], 2)
+        product_b(b13_ps[:, 0, :], 1)
+        product_b(b13_ps[:, 1, :], 3)
+        scalar_copy(read[0][:], pw[0][:].indirect(list5[:]))
+        scalar_copy(read[2][:], pw[2][:].indirect(list5[:]))
+        scalar_copy(b13[:], b13_ps[:])
+        scalar_copy(pv[1][:].indirect(list4[:]), b13[:, 0, :])
+        scalar_copy(read[1][:], pv[1][:].indirect(list6[:]))
+        scalar_copy(pv[3][:].indirect(list4[:]), b13[:, 1, :])
+        for h in range(2):
+            scalar_copy(read[3][:, halves[h]], pv[3][:].indirect(list6[:, 8 * h : 8 * h + 8]))
+
+        wb_dealt = tile("wb_dealt", [P, PACK, P], U32)
+        deal(nc.vector.tensor_copy, wb_dealt[:], wb_raw[:], 4)
+        ws_plane_dealt = tile("ws_plane_dealt", [P, PACK, P], U8)
+        wb_plane_dealt = tile("wb_plane_dealt", [P, PACK, P], U8)
+        deal(nc.vector.tensor_copy, ws_plane_dealt[:], ws_plane[:], 16)
+        deal(nc.vector.tensor_copy, wb_plane_dealt[:], wb_plane[:], 16)
+        b02 = shared("b02", [P, 2, SLOTS], F32, "b02")
+        nc.vector.tensor_copy(b02[:], b02_ps[:])
+        nc.vector.tensor_copy(pv[0][:].indirect(list4[:]), b02[:, 0, :])
+        nc.vector.tensor_copy(pv[2][:].indirect(list4[:]), b02[:, 1, :])
+
+        y_ps = [
+            [ps.tile([P, 2, HALF], F32, name="y_ps%d%d" % (h, u), tag="first" if h + u == 2 else "y%d%d" % (h, u)) for u in range(2)]
+            for h in range(2)
+        ]
         for h in range(2):
             for t in range(PACK):
                 nc.tensor.matmul_mx(
-                    y_ps[h][:, t, :], ws_dealt[:, t, :].bitcast(E5M2), ws_plane_dealt[:, t, :],
-                    sx[:, halves[h]].bitcast(E2M1), sx_plane[:, halves[h]], start=(t == 0), stop=False,
+                    y_ps[h][t // 2][:, t % 2, :], ws_dealt[:, t, :].bitcast(E5M2), ws_plane_dealt[:, t, :],
+                    sx[:, halves[h]].bitcast(E2M1), sx_plane[:, halves[h]], start=(t % 2 == 0), stop=False,
                 )
 
-        last = PACK - 1
+        diff = shared("diff", [P, 2, PACK, HALF], F32, "b02")
         for h in range(2):
-            nc.vector.tensor_tensor(
-                diff[:, last, halves[h]], pv[last][:].indirect(list6[:, 8 * h : 8 * h + 8]),
-                pw_read[last][:, halves[h]], ALU.subtract,
-            )
+            for t in (0, 2, 1, 3):
+                board, places = (pv[t], list6) if t % 2 == 0 else (pw[t], list5)
+                nc.vector.tensor_tensor(
+                    diff[:, h, t, :], board[:].indirect(places[:, 8 * h : 8 * h + 8]),
+                    read[t][:, halves[h]], ALU.subtract,
+                )
         hid = [tile("hid%d" % h, [P, HALF, PACK], BF16) for h in range(2)]
         for h in range(2):
             nc.scalar.activation(
                 hid[h][:].rearrange("p (c i) t -> p c t i", i=4),
-                diff[:, :, halves[h]].rearrange("p t (c i) -> p c t i", i=4),
+                diff[:, h].rearrange("p t (c i) -> p c t i", i=4),
                 ACT.Abs,
             )
         for h in range(2):
@@ -205,8 +217,8 @@ def tile_list_ahead_twoboards_skip_plain_pl_kernel(
             )
             for t in range(PACK):
                 nc.tensor.matmul_mx(
-                    y_ps[h][:, t, :], wb_dealt[:, t, :].bitcast(E5M2), wb_plane_dealt[:, t, :],
-                    hid_codes[:].bitcast(E4M3), hid_plane[:], start=False, stop=(t == last),
+                    y_ps[h][t // 2][:, t % 2, :], wb_dealt[:, t, :].bitcast(E5M2), wb_plane_dealt[:, t, :],
+                    hid_codes[:].bitcast(E4M3), hid_plane[:], start=False, stop=(t % 2 == 1),
                 )
 
         y_codes = tile("y_codes", [P, READS], U32)
@@ -216,7 +228,8 @@ def tile_list_ahead_twoboards_skip_plain_pl_kernel(
         for h in range(2):
             y_bf = tile("y_bf%d" % h, [P, HALF, PACK], BF16)
             y = tile("y%d" % h, [P, PACK, HALF], F32)
-            scalar_copy(y[:], y_ps[h][:])
+            for u in range(2):
+                scalar_copy(y[:, 2 * u : 2 * u + 2, :], y_ps[h][u][:])
             nc.vector.tensor_copy(
                 y_bf[:].rearrange("p (c i) t -> p c t i", i=4), y[:].rearrange("p t (c i) -> p c t i", i=4)
             )
@@ -226,4 +239,4 @@ def tile_list_ahead_twoboards_skip_plain_pl_kernel(
             nc.scalar.dma_start(out_rows[:, :, halves[h]], y[:])
             nc.sync.dma_start(out_words[:, halves[h]], y_codes[:, halves[h]].bitcast(I32))
         for r in range(4):
-            nc.sync.dma_start(out_2[0, r:16:4, :].bitcast(I32), y_plane[r:P:32, :].bitcast(I32))
+            (nc.sync if r < 2 else nc.scalar).dma_start(out_2[0, r:16:4, :].bitcast(I32), y_plane[r:P:32, :].bitcast(I32))

@@ -62,7 +62,7 @@ def tile_list_ahead_twoboards_skip_plain_pl_kernel(
         w_plane = tile("w_plane", [P, WIDTH], U8)
         w2_plane = tile("w2_plane", [P, WIDTH], U8)
         ws_plane = tile("ws_plane", [P, WIDTH], U8)
-        wb_plane = shared("wb_plane", [P, WIDTH], U8, "b02")
+        wb_plane = tile("wb_plane", [P, WIDTH], U8)
         sx_plane = tile("sx_plane", [P, READS], U8)
         nc.gpsimd.memset(w_plane[:].bitcast(I32), 0)
         nc.vector.memset(xt_plane[:, : TOKENS // 2].bitcast(I32), 0)
@@ -163,7 +163,7 @@ def tile_list_ahead_twoboards_skip_plain_pl_kernel(
         product_b(b02_ps[:, 1, :], 2)
         product_b(b13_ps[:, 0, :], 1)
         product_b(b13_ps[:, 1, :], 3)
-        scalar_copy(read[0][:], pw[0][:].indirect(list5[:]))
+        nc.vector.tensor_copy(read[0][:], pw[0][:].indirect(list5[:]))
         scalar_copy(read[2][:], pw[2][:].indirect(list5[:]))
         scalar_copy(b13[:], b13_ps[:])
         scalar_copy(pv[1][:].indirect(list4[:]), b13[:, 0, :])
@@ -173,11 +173,11 @@ def tile_list_ahead_twoboards_skip_plain_pl_kernel(
             scalar_copy(read[3][:, halves[h]], pv[3][:].indirect(list6[:, 8 * h : 8 * h + 8]))
 
         wb_dealt = tile("wb_dealt", [P, PACK, P], U32)
-        deal(nc.vector.tensor_copy, wb_dealt[:], wb_raw[:], 4)
+        deal(nc.gpsimd.tensor_copy, wb_dealt[:], wb_raw[:], 4)
         ws_plane_dealt = tile("ws_plane_dealt", [P, PACK, P], U8)
         wb_plane_dealt = tile("wb_plane_dealt", [P, PACK, P], U8)
-        deal(nc.vector.tensor_copy, ws_plane_dealt[:], ws_plane[:], 16)
-        deal(nc.vector.tensor_copy, wb_plane_dealt[:], wb_plane[:], 16)
+        deal(nc.gpsimd.tensor_copy, ws_plane_dealt[:], ws_plane[:], 16)
+        deal(nc.gpsimd.tensor_copy, wb_plane_dealt[:], wb_plane[:], 16)
         b02 = shared("b02", [P, 2, SLOTS], F32, "b02")
         nc.vector.tensor_copy(b02[:], b02_ps[:])
         nc.vector.tensor_copy(pv[0][:].indirect(list4[:]), b02[:, 0, :])

@@ -105,8 +105,10 @@ def tile_list_ahead_twoboards_skip_plain_pl_kernel(
         w2_dealt = tile("w2_dealt", [P, PACK, P], U32)
         ws_dealt = tile("ws_dealt", [P, PACK, P], U32)
         deal(nc.scalar.copy, w_dealt[:], w_raw[:], 8)
-        deal(nc.scalar.copy, w2_dealt[:], w2_raw[:], 4)
-        deal(nc.scalar.copy, ws_dealt[:], ws_raw[:], 4)
+        w2_plane_dealt = tile("w2_plane_dealt", [P, PACK, P], U8)
+        deal(nc.gpsimd.tensor_copy, w2_dealt[:], w2_raw[:], 4)
+        deal(nc.gpsimd.tensor_copy, w2_plane_dealt[:], w2_plane[:], 16)
+        deal(nc.gpsimd.tensor_copy, ws_dealt[:], ws_raw[:], 4)
         x1 = tile("x1", [P, SLOTS], U32)
         x1_plane = tile("x1_plane", [P, SLOTS], U8)
         x2 = tile("x2", [P, SLOTS], U32)
@@ -139,7 +141,7 @@ def tile_list_ahead_twoboards_skip_plain_pl_kernel(
         b02_ps = ps.tile([P, 2, SLOTS], F32, name="b02_ps")
         b13_ps = ps.tile([P, 2, SLOTS], F32, name="b13_ps")
         a0 = tile("a0", [P, SLOTS], F32)
-        a1 = shared("a1", [P, SLOTS], F32, "a1")
+        a1 = tile("a1", [P, SLOTS], F32)
         a23 = tile("a23", [P, 2, SLOTS], F32)
         b13 = tile("b13", [P, 2, SLOTS], F32)
         read = [tile("read%d" % t, [P, READS], F32) for t in range(PACK)]
@@ -153,8 +155,6 @@ def tile_list_ahead_twoboards_skip_plain_pl_kernel(
         scalar_copy(pw[0][:].indirect(list3[:]), a0[:])
         nc.vector.tensor_copy(a1[:], a1_ps[:])
         nc.vector.tensor_copy(pw[1][:].indirect(list3[:]), a1[:])
-        w2_plane_dealt = shared("w2_plane_dealt", [P, PACK, P], U8, "a1")
-        deal(nc.vector.tensor_copy, w2_plane_dealt[:], w2_plane[:], 16)
         scalar_copy(a23[:], a23_ps[:])
         scalar_copy(pw[2][:].indirect(list3[:]), a23[:, 0, :])
         nc.vector.tensor_copy(pw[3][:].indirect(list3[:]), a23[:, 1, :])

from contextlib import ExitStack

import concourse.mybir as mybir

F32 = mybir.dt.float32
BF16 = mybir.dt.bfloat16
I32 = mybir.dt.int32
U32 = mybir.dt.uint32
U16 = mybir.dt.uint16
U8 = mybir.dt.uint8
E4M3 = mybir.dt.float8_e4m3fn_x4
E5M2 = mybir.dt.float8_e5m2_x4
E2M1 = mybir.dt.float4_e2m1fn_x4
ACT = mybir.ActivationFunctionType
ALU = mybir.AluOpType

P = 128
PACK = 4
TOKENS, SLOTS, BOARD, READS, WIDTH = 2048, 256, 512, 256, 512
HALF = READS // 2
FLOPS = 536870912


def tile_list_ahead_twoboards_skip_plain_pl_kernel(
    tc, xt_words, xt_scales, w_words, w_scales, w2_words, w2_scales, wb_words, wb_scales,
    sx_words, sx_scales, ws_words, ws_scales, offs, offs2, offs3, offs4, offs5, offs6,
    out_0, out_1, out_2,
):
    nc = tc.nc
    with ExitStack() as ctx:
        sb = ctx.enter_context(tc.tile_pool(name="sb", bufs=1))
        ps = ctx.enter_context(tc.psum_pool(name="ps", bufs=1))

        def tile(name, shape, dtype):
            return sb.tile(shape, dtype, name=name, align_bytes=64)

        def load_list(name, src):
            dst = sb.tile([P, 16], U16, name=name)
            nc.sync.dma_start(dst[:], src)
            return dst

        def load_words(dst, src):
            nc.sync.dma_start(dst.bitcast(I32), src.bitcast(I32))

        def words8(src):
            return src[0].rearrange("p n t -> p (n t)")

        def load_plane(dst, src):
            for r in range(4):
                nc.sync.dma_start(dst[r:P:32, :].bitcast(I32), src[0, r:16:4, :].bitcast(I32))

        def deal(copy, dst, src, run):
            copy(
                dst.rearrange("p t (c i) -> p c t i", i=run),
                src.rearrange("p (c i t) -> p c t i", i=run, t=PACK),
            )

        def shared(name, shape, dtype, tag):
            return sb.tile(shape, dtype, name=name, tag=tag, align_bytes=64)

        xt_plane = tile("xt_plane", [P, TOKENS], U8)
        w_plane = tile("w_plane", [P, WIDTH], U8)
        w2_plane = tile("w2_plane", [P, WIDTH], U8)
        ws_plane = tile("ws_plane", [P, WIDTH], U8)
        wb_plane = tile("wb_plane", [P, WIDTH], U8)
        sx_plane = tile("sx_plane", [P, READS], U8)
        nc.gpsimd.memset(w_plane[:].bitcast(I32), 0)
        nc.vector.memset(xt_plane[:, : TOKENS // 2].bitcast(I32), 0)
        nc.gpsimd.memset(xt_plane[:, TOKENS // 2 :].bitcast(I32), 0)
        for plane in (w2_plane, ws_plane, wb_plane, sx_plane):
            nc.vector.memset(plane[:].bitcast(I32), 0)
        pw = [tile("pw%d" % t, [P, BOARD], F32) for t in range(PACK)]
        pv = [tile("pv%d" % t, [P, BOARD], F32) for t in range(PACK)]
        for t in range(PACK):
            nc.vector.memset(pw[t][:], 0.0)
        for t in range(PACK):
            (nc.vector if t < 2 else nc.gpsimd).memset(pv[t][:], 0.0)

        w_raw = tile("w_raw", [P, WIDTH], U16)
        xt = tile("xt", [P, TOKENS], U32)
        w2_raw = tile("w2_raw", [P, WIDTH], U32)
        ws_raw = tile("ws_raw", [P, WIDTH], U32)
        wb_raw = tile("wb_raw", [P, WIDTH], U32)
        sx = tile("sx", [P, READS], U16)
        list1 = load_list("list1", offs)
        load_words(w_raw[:], w_words[0])
        list3 = load_list("list3", offs3)
        load_plane(w_plane, w_scales)
        load_words(xt[:], words8(xt_words))
        load_plane(xt_plane, xt_scales)
        list2 = load_list("list2", offs2)
        load_words(w2_raw[:], words8(w2_words))
        load_words(ws_raw[:], words8(ws_words))
        load_plane(w2_plane, w2_scales)
        list5 = load_list("list5", offs5)
        list4 = load_list("list4", offs4)
        list6 = load_list("list6", offs6)
        load_words(wb_raw[:], words8(wb_words))
        load_plane(ws_plane, ws_scales)
        load_plane(wb_plane, wb_scales)
        load_words(sx[:], sx_words[0])
        load_plane(sx_plane, sx_scales)

        w_dealt = tile("w_dealt", [P, PACK, P], U16)
        w2_dealt = tile("w2_dealt", [P, PACK, P], U32)
        ws_dealt = tile("ws_dealt", [P, PACK, P], U32)
        deal(nc.scalar.copy, w_dealt[:], w_raw[:], 8)
        w2_plane_dealt = tile("w2_plane_dealt", [P, PACK, P], U8)
        deal(nc.gpsimd.tensor_copy, w2_dealt[:], w2_raw[:], 4)
        deal(nc.gpsimd.tensor_copy, w2_plane_dealt[:], w2_plane[:], 16)
        deal(nc.gpsimd.tensor_copy, ws_dealt[:], ws_raw[:], 4)
        x1 = tile("x1", [P, SLOTS], U32)
        x1_plane = tile("x1_plane", [P, SLOTS], U8)
        x2 = tile("x2", [P, SLOTS], U32)
        x2_plane = tile("x2_plane", [P, SLOTS], U8)
        w_plane_dealt = tile("w_plane_dealt", [P, PACK, P], U8)
        deal(nc.vector.tensor_copy, w_plane_dealt[:], w_plane[:], 16)
        nc.vector.tensor_copy(x1_plane[:], xt_plane[:].indirect(list1[:]))
        nc.vector.tensor_copy(x1[:], xt[:].indirect(list1[:]))
        nc.vector.tensor_copy(x2_plane[:], xt_plane[:].indirect(list2[:]))
        nc.vector.tensor_copy(x2[:], xt[:].indirect(list2[:]))

        def scalar_copy(dst, src):
            nc.scalar.activation(dst, src, ACT.Copy)

        def product_a(acc, t):
            nc.tensor.matmul_mx(
                acc, w_dealt[:, t, :].bitcast(E2M1), w_plane_dealt[:, t, :],
                x1[:].bitcast(E4M3), x1_plane[:], start=True, stop=True,
            )

        def product_b(acc, t):
            nc.tensor.matmul_mx(
                acc, w2_dealt[:, t, :].bitcast(E5M2), w2_plane_dealt[:, t, :],
                x2[:].bitcast(E4M3), x2_plane[:], start=True, stop=True,
            )

        a0_ps = ps.tile([P, SLOTS], F32, name="a0_ps", tag="first")
        a1_ps = ps.tile([P, SLOTS], F32, name="a1_ps")
        a23_ps = ps.tile([P, 2, SLOTS], F32, name="a23_ps")
        b02_ps = ps.tile([P, 2, SLOTS], F32, name="b02_ps")
        b13_ps = ps.tile([P, 2, SLOTS], F32, name="b13_ps")
        a0 = tile("a0", [P, SLOTS], F32)
        a1 = tile("a1", [P, SLOTS], F32)
        a23 = tile("a23", [P, 2, SLOTS], F32)
        b13 = tile("b13", [P, 2, SLOTS], F32)
        read = [tile("read%d" % t, [P, READS], F32) for t in range(PACK)]
        halves = [slice(h * HALF, (h + 1) * HALF) for h in range(2)]

        product_a(a0_ps[:], 0)
        product_a(a1_ps[:], 1)
        product_a(a23_ps[:, 0, :], 2)
        product_a(a23_ps[:, 1, :], 3)
        scalar_copy(a0[:], a0_ps[:])
        scalar_copy(pw[0][:].indirect(list3[:]), a0[:])
        nc.vector.tensor_copy(a1[:], a1_ps[:])
        nc.vector.tensor_copy(pw[1][:].indirect(list3[:]), a1[:])
        scalar_copy(a23[:], a23_ps[:])
        scalar_copy(pw[2][:].indirect(list3[:]), a23[:, 0, :])
        nc.vector.tensor_copy(pw[3][:].indirect(list3[:]), a23[:, 1, :])

        product_b(b02_ps[:, 0, :], 0)
        product_b(b02_ps[:, 1, :], 2)
        product_b(b13_ps[:, 0, :], 1)
        product_b(b13_ps[:, 1, :], 3)
        nc.vector.tensor_copy(read[0][:], pw[0][:].indirect(list5[:]))
        scalar_copy(read[2][:], pw[2][:].indirect(list5[:]))
        scalar_copy(b13[:], b13_ps[:])
        scalar_copy(pv[1][:].indirect(list4[:]), b13[:, 0, :])
        scalar_copy(read[1][:], pv[1][:].indirect(list6[:]))
        scalar_copy(pv[3][:].indirect(list4[:]), b13[:, 1, :])
        for h in range(2):
            scalar_copy(read[3][:, halves[h]], pv[3][:].indirect(list6[:, 8 * h : 8 * h + 8]))

        wb_dealt = tile("wb_dealt", [P, PACK, P], U32)
        deal(nc.gpsimd.tensor_copy, wb_dealt[:], wb_raw[:], 4)
        ws_plane_dealt = tile("ws_plane_dealt", [P, PACK, P], U8)
        wb_plane_dealt = tile("wb_plane_dealt", [P, PACK, P], U8)
        deal(nc.gpsimd.tensor_copy, ws_plane_dealt[:], ws_plane[:], 16)
        deal(nc.gpsimd.tensor_copy, wb_plane_dealt[:], wb_plane[:], 16)
        b02 = shared("b02", [P, 2, SLOTS], F32, "b02")
        nc.vector.tensor_copy(b02[:], b02_ps[:])
        nc.vector.tensor_copy(pv[0][:].indirect(list4[:]), b02[:, 0, :])
        nc.vector.tensor_copy(pv[2][:].indirect(list4[:]), b02[:, 1, :])

        y_ps = [
            [ps.tile([P, 2, HALF], F32, name="y_ps%d%d" % (h, u), tag="first" if h + u == 2 else "y%d%d" % (h, u)) for u in range(2)]
            for h in range(2)
        ]
        for h in range(2):
            for t in range(PACK):
                nc.tensor.matmul_mx(
                    y_ps[h][t // 2][:, t % 2, :], ws_dealt[:, t, :].bitcast(E5M2), ws_plane_dealt[:, t, :],
                    sx[:, halves[h]].bitcast(E2M1), sx_plane[:, halves[h]], start=(t % 2 == 0), stop=False,
                )

        diff = shared("diff", [P, 2, PACK, HALF], F32, "b02")
        for h in range(2):
            for t in (0, 2, 1, 3):
                board, places = (pv[t], list6) if t % 2 == 0 else (pw[t], list5)
                nc.vector.tensor_tensor(
                    diff[:, h, t, :], board[:].indirect(places[:, 8 * h : 8 * h + 8]),
                    read[t][:, halves[h]], ALU.subtract,
                )
        hid = [tile("hid%d" % h, [P, HALF, PACK], BF16) for h in range(2)]
        for h in range(2):
            nc.scalar.activation(
                hid[h][:].rearrange("p (c i) t -> p c t i", i=4),
                diff[:, h].rearrange("p t (c i) -> p c t i", i=4),
                ACT.Abs,
            )
        for h in range(2):
            hid_codes = tile("hid_codes%d" % h, [P, HALF], U32)
            hid_plane = tile("hid_plane%d" % h, [P, HALF], U8)
            nc.vector.quantize_mx(
                hid_codes[:].bitcast(E4M3), hid_plane[:], hid[h][:].rearrange("p o t -> p (o t)")
            )
            for t in range(PACK):
                nc.tensor.matmul_mx(
                    y_ps[h][t // 2][:, t % 2, :], wb_dealt[:, t, :].bitcast(E5M2), wb_plane_dealt[:, t, :],
                    hid_codes[:].bitcast(E4M3), hid_plane[:], start=False, stop=(t % 2 == 1),
                )

        y_codes = tile("y_codes", [P, READS], U32)
        y_plane = tile("y_plane", [P, READS], U8)
        out_rows = out_0.rearrange("(p t) o -> p t o", t=PACK)
        out_words = out_1[0].rearrange("p o t -> p (o t)").bitcast(I32)
        for h in range(2):
            y_bf = tile("y_bf%d" % h, [P, HALF, PACK], BF16)
            y = tile("y%d" % h, [P, PACK, HALF], F32)
            for u in range(2):
                scalar_copy(y[:, 2 * u : 2 * u + 2, :], y_ps[h][u][:])
            nc.vector.tensor_copy(
                y_bf[:].rearrange("p (c i) t -> p c t i", i=4), y[:].rearrange("p t (c i) -> p c t i", i=4)
            )
            nc.vector.quantize_mx(
                y_codes[:, halves[h]].bitcast(E4M3), y_plane[:, halves[h]], y_bf[:].rearrange("p o t -> p (o t)")
            )
            nc.scalar.dma_start(out_rows[:, :, halves[h]], y[:])
            nc.sync.dma_start(out_words[:, halves[h]], y_codes[:, halves[h]].bitcast(I32))
        for r in range(4):
            (nc.sync if r < 2 else nc.scalar).dma_start(out_2[0, r:16:4, :].bitcast(I32), y_plane[r:P:32, :].bitcast(I32))
